import numpy as np
import ml_dtypes


def mxq(x, axis, fmt="e4m3"):
    dtype, down = {"e4m3": (ml_dtypes.float8_e4m3fn, 7), "e5m2": (ml_dtypes.float8_e5m2, 14)}[fmt]
    v = np.moveaxis(np.asarray(x, np.float32).astype(ml_dtypes.bfloat16).astype(np.float64), axis, -1)
    blocks = v.reshape(v.shape[:-1] + (-1, 32))
    amax = np.abs(blocks).max(-1, keepdims=True)
    byte = np.maximum(np.where(amax > 0, np.frexp(amax)[1] - 1 + 127, 0) - down, 1)
    scale = np.exp2(byte - 127.0)
    codes = (blocks / scale).astype(np.float32).astype(dtype).astype(np.float64)
    return np.moveaxis((codes * scale).reshape(v.shape), -1, axis)


WIDE = False


def mx_kscale(k):
    if not WIDE:
        return np.ones(k)
    levels = np.array([10, -10, 5, -5, 0])
    if k % 512:
        return np.exp2(np.random.permutation(np.resize(levels, k // 32))).repeat(32)
    a = np.empty((k // 512, 16))
    for p in range(k // 512):
        a[p, :8] = np.random.permutation(np.resize(levels, 8))
        for g in range(8):
            far = levels[np.abs(levels - a[p, g]) >= 10]
            a[p, g + 8] = far[np.random.randint(len(far))]
    return np.exp2(a.ravel()).repeat(32)


def f64(x):
    return np.asarray(x).astype(np.float64)


def striped8(idx):
    return np.asarray(idx).reshape(8, -1, 16).transpose(0, 2, 1).reshape(128, -1).astype(np.uint16)


def unstriped8(offs):
    return offs.reshape(8, 16, -1).transpose(0, 2, 1).reshape(8, -1).astype(np.int64)


def pick8(x, idx, run):
    r = np.arange(len(x))
    return x[r[:, None], idx[r % (8 * run) // run]]


E2M1 = np.array([0.0, 0.5, 1.0, 1.5, 2.0, 3.0, 4.0, 6.0, -0.0, -0.5, -1.0, -1.5, -2.0, -3.0, -4.0, -6.0])


def pack_weight(w, fmt):
    k, n = w.shape
    w = f64(np.asarray(w, np.float32).astype(ml_dtypes.bfloat16)).reshape(k // 32, 32, n)
    amax = np.abs(w).max(1)
    if fmt == "e4m3":
        byte = np.frexp(amax)[1] - 1 + 127 - 7
    else:
        mant, ex = np.frexp(amax / 6.0)
        byte = np.where(mant > 0.5, ex, ex - 1) + 127
    byte = np.clip(np.where(amax > 0, byte, 1), 1, 254)
    scaled = (w * np.exp2(127.0 - byte)[:, None, :]).reshape(k, n).astype(np.float32)
    by_word = np.ascontiguousarray(scaled.reshape(k // 512, 128, 4, n).transpose(0, 1, 3, 2))
    if fmt == "e4m3":
        words = by_word.astype(ml_dtypes.float8_e4m3fn).view(np.uint8)
    else:
        c = by_word.astype(ml_dtypes.float4_e2m1fn).view(np.uint8) & 0xF
        words = (c[..., 0::2] | (c[..., 1::2] << 4)).reshape(k // 512, 128, 2 * n)
    return np.ascontiguousarray(words), np.ascontiguousarray(byte.astype(np.uint8).reshape(k // 512, 16, n))


def unpack_weight(words, scales, fmt):
    g, _, n = scales.shape
    words = np.ascontiguousarray(words).reshape(g, 128, n, -1)
    if fmt == "e4m3":
        vals = words.view(ml_dtypes.float8_e4m3fn).astype(np.float64)
    else:
        nib = np.empty((g, 128, n, 4), np.uint8)
        nib[..., 0::2] = words & 0xF
        nib[..., 1::2] = words >> 4
        vals = E2M1[nib]
    vals = vals * np.repeat(np.exp2(scales.astype(np.float64) - 127.0), 8, axis=1)[..., None]
    return vals.transpose(0, 1, 3, 2).reshape(g * 512, n)


D, T, U, I, Q = 512, 1024, 1024, 512, 128


def setup_inputs():
    n = np.random.standard_normal
    idx = np.stack([np.random.permutation(T)[:I] for _ in range(8)])
    idx2 = np.stack([np.random.permutation(U)[:I] for _ in range(8)])
    idx3 = np.stack([np.random.permutation(U)[:I] for _ in range(8)])
    idx4 = np.stack([np.random.permutation(U)[:I] for _ in range(8)])
    idx5 = np.stack([np.random.permutation(T)[:I] for _ in range(8)])
    fd = mx_kscale(D)
    cachep = pack_weight(n((D, T)) / fd[:, None], "e2m1")
    draftp = pack_weight(n((D, U)) / fd[:, None], "e4m3")
    return {
        "query": (n((D, Q)) * 1.0 / np.sqrt(D) * fd[:, None]).astype(np.float32),
        "cache_words": cachep[0],
        "cache_scales": cachep[1],
        "draft_words": draftp[0],
        "draft_scales": draftp[1],
        "offs": striped8(idx),
        "offs2": striped8(idx2),
        "offs3": striped8(idx3),
        "offs4": striped8(idx4),
        "offs5": striped8(idx5),
    }


def reference(query, cache_words, cache_scales, draft_words, draft_scales, offs, offs2, offs3, offs4, offs5):
    idx = unstriped8(offs)
    idx2 = unstriped8(offs2)
    idx3 = unstriped8(offs3)
    idx4 = unstriped8(offs4)
    idx5 = unstriped8(offs5)
    cacheu = unpack_weight(cache_words, cache_scales, "e2m1")
    draftu = unpack_weight(draft_words, draft_scales, "e4m3")
    queryq = mxq(f64(query), 0, "e4m3")
    a = queryq.T @ cacheu
    b = queryq.T @ draftu
    f1 = np.zeros((Q, U))
    f1[np.arange(Q)[:, None], idx2[np.arange(Q) % 128 // 16]] = pick8(a, idx, 16)
    f2 = np.zeros((Q, U))
    f2[np.arange(Q)[:, None], idx3[np.arange(Q) % 128 // 16]] = pick8(a, idx, 16)
    r = f1 - f2
    bb = np.maximum(b, r)
    y = pick8(bb, idx4, 16) - pick8(a, idx5, 16)
    return y

@@ -1,0 +1,128 @@
+from contextlib import ExitStack
+
+import concourse.mybir as mybir
+
+F32 = mybir.dt.float32
+BF16 = mybir.dt.bfloat16
+I32 = mybir.dt.int32
+U32 = mybir.dt.uint32
+U16 = mybir.dt.uint16
+U8 = mybir.dt.uint8
+FP8X4 = mybir.dt.float8_e4m3fn_x4
+FP4X4 = mybir.dt.float4_e2m1fn_x4
+COPY = mybir.ActivationFunctionType.Copy
+SUB = mybir.AluOpType.subtract
+MAX = mybir.AluOpType.max
+
+P = 128
+D, T, U, I, Q = 512, 1024, 1024, 512, 128
+FLOPS = 2 * Q * D * (T + U)
+
+
+def load_scales(nc, queue, plane, scales):
+    for quad in range(4):
+        queue.dma_start(
+            out=plane[32 * quad : 32 * quad + 4, :].bitcast(I32),
+            in_=scales[0, 4 * quad : 4 * quad + 4, :].bitcast(I32),
+        )
+
+
+def tile_attend_bothsides_two_kernel(tc, query, cache_words, cache_scales, draft_words, draft_scales, offs, offs2, offs3, offs4, offs5, out):
+    nc = tc.nc
+    with ExitStack() as ctx:
+        sb = ctx.enter_context(tc.tile_pool(name="sb", bufs=1))
+        ps = ctx.enter_context(tc.psum_pool(name="ps", bufs=1))
+
+        c_plane = sb.tile([P, T], U8, name="c_plane", align_bytes=64)
+        d_plane = sb.tile([P, U], U8, name="d_plane", align_bytes=64)
+
+        q_raw = sb.tile([P, 4, Q], F32, name="q_raw")
+        nc.sync.dma_start(out=q_raw[:], in_=query.rearrange("(p j) w -> p j w", j=4))
+        c_words = sb.tile([P, 2 * T], U8, name="c_words", align_bytes=64)
+        nc.sync.dma_start(out=c_words[:].bitcast(I32), in_=cache_words[0].bitcast(I32))
+        load_scales(nc, nc.sync, c_plane, cache_scales)
+        lists = []
+        for name, src in (("l1", offs), ("l2", offs2), ("l3", offs3)):
+            lst = sb.tile([P, I // 16], U16, name=name)
+            nc.sync.dma_start(lst[:], src)
+            lists.append(lst)
+        load_scales(nc, nc.sync, d_plane, draft_scales)
+        d_words = sb.tile([P, U], U32, name="d_words", align_bytes=64)
+        nc.sync.dma_start(out=d_words[:].bitcast(I32), in_=draft_words[0].rearrange("p n t -> p (n t)").bitcast(I32))
+        for name, src in (("l5", offs5), ("l4", offs4)):
+            lst = sb.tile([P, I // 16], U16, name=name)
+            nc.sync.dma_start(lst[:], src)
+            lists.append(lst)
+        l1, l2, l3, l5, l4 = lists
+
+        f1 = sb.tile([P, U], F32, name="f1")
+        f2 = sb.tile([P, U], F32, name="f2")
+        nc.vector.memset(f1[:], 0.0)
+        nc.vector.memset(f2[:], 0.0)
+
+        q_bf = sb.tile([P, Q, 4], BF16, name="q_bf", align_bytes=64)
+        nc.vector.tensor_copy(out=q_bf[:], in_=q_raw[:].rearrange("p j w -> p w j"))
+        q_codes = sb.tile([P, Q], U32, name="q_codes", align_bytes=64)
+        q_plane = sb.tile([P, Q], U8, name="q_plane", align_bytes=64)
+        nc.vector.quantize_mx(out=q_codes[:].bitcast(FP8X4), scales=q_plane[:], in_=q_bf[:].rearrange("p w j -> p (w j)"))
+
+        a = sb.tile([P, T], F32, name="a")
+        start = 0
+        for n, width in enumerate((256, 256, 256, 128, 128)):
+            bank = ps.tile([P, width], F32, name="a_bank%d" % n)
+            nc.tensor.matmul_mx(
+                out=bank[:],
+                lhsT=q_codes[:].bitcast(FP8X4),
+                lhsT_scale=q_plane[:],
+                rhs=c_words[:, 2 * start : 2 * (start + width)].bitcast(FP4X4),
+                rhs_scale=c_plane[:, start : start + width],
+                start=True,
+                stop=True,
+            )
+            if n % 2 == 0:
+                nc.scalar.activation(a[:, start : start + width], bank[:], COPY)
+            else:
+                nc.vector.tensor_copy(out=a[:, start : start + width], in_=bank[:])
+            start += width
+
+        b_banks = []
+        for n in range(2):
+            bank = ps.tile([P, 512], F32, name="b_bank%d" % n)
+            nc.tensor.matmul_mx(
+                out=bank[:],
+                lhsT=q_codes[:].bitcast(FP8X4),
+                lhsT_scale=q_plane[:],
+                rhs=d_words[:, 512 * n : 512 * (n + 1)].bitcast(FP8X4),
+                rhs_scale=d_plane[:, 512 * n : 512 * (n + 1)],
+                start=True,
+                stop=True,
+            )
+            b_banks.append(bank)
+
+        picked = sb.tile([P, I], F32, name="picked")
+        for h in range(2):
+            nc.vector.tensor_copy(picked[:, 256 * h : 256 * (h + 1)], a[:].indirect(l1[:, 16 * h : 16 * (h + 1)]))
+        for h in range(2):
+            nc.scalar.activation(f1[:].indirect(l2[:, 16 * h : 16 * (h + 1)]), picked[:, 256 * h : 256 * (h + 1)], COPY)
+            nc.scalar.activation(f2[:].indirect(l3[:, 16 * h : 16 * (h + 1)]), picked[:, 256 * h : 256 * (h + 1)], COPY)
+
+        minus = sb.tile([P, I], F32, name="minus")
+        nc.vector.tensor_copy(minus[:], a[:].indirect(l5[:]))
+
+        r = sb.tile([P, U], F32, name="r")
+        bb = sb.tile([P, U], F32, name="bb")
+        for n in range(2):
+            cols = slice(512 * n, 512 * (n + 1))
+            nc.vector.tensor_tensor(r[:, cols], f1[:, cols], f2[:, cols], SUB)
+        for n in range(2):
+            cols = slice(512 * n, 512 * (n + 1))
+            nc.vector.tensor_tensor(bb[:, cols], b_banks[n][:], r[:, cols], MAX)
+
+        y0 = sb.tile([P, 256], F32, name="y0")
+        y1 = sb.tile([P, 256], F32, name="y1")
+        g1 = sb.tile([P, 256], F32, name="g1")
+        nc.vector.tensor_tensor(y0[:], bb[:].indirect(l4[:, 0:16]), minus[:, 0:256], SUB)
+        nc.scalar.activation(g1[:], bb[:].indirect(l4[:, 16:32]), COPY)
+        nc.vector.tensor_tensor(y1[:], g1[:], minus[:, 256:512], SUB)
+        nc.sync.dma_start(out=out[:, 0:256], in_=y0[:])
+        nc.sync.dma_start(out=out[:, 256:512], in_=y1[:])

@@ -42,14 +42,14 @@ def tile_attend_bothsides_two_kernel(tc, query, cache_words, cache_scales, draft
         nc.sync.dma_start(out=c_words[:].bitcast(I32), in_=cache_words[0].bitcast(I32))
         load_scales(nc, nc.sync, c_plane, cache_scales)
         lists = []
-        for name, src in (("l1", offs), ("l2", offs2), ("l3", offs3)):
+        for name, src in (("l1", offs), ("l2", offs2), ("l3", offs3), ("l5", offs5)):
             lst = sb.tile([P, I // 16], U16, name=name)
             nc.sync.dma_start(lst[:], src)
             lists.append(lst)
         load_scales(nc, nc.sync, d_plane, draft_scales)
         d_words = sb.tile([P, U], U32, name="d_words", align_bytes=64)
         nc.sync.dma_start(out=d_words[:].bitcast(I32), in_=draft_words[0].rearrange("p n t -> p (n t)").bitcast(I32))
-        for name, src in (("l5", offs5), ("l4", offs4)):
+        for name, src in (("l4", offs4),):
             lst = sb.tile([P, I // 16], U16, name=name)
             nc.sync.dma_start(lst[:], src)
             lists.append(lst)
@@ -109,7 +109,7 @@ def tile_attend_bothsides_two_kernel(tc, query, cache_words, cache_scales, draft
         minus = sb.tile([P, I], F32, name="minus")
         nc.vector.tensor_copy(minus[:], a[:].indirect(l5[:]))
 
-        r = sb.tile([P, U], F32, name="r")
+        r = sb.tile([P, U], F32, name="r", tag="a")
         bb = sb.tile([P, U], F32, name="bb")
         for n in range(2):
             cols = slice(512 * n, 512 * (n + 1))

@@ -102,21 +102,37 @@ def tile_attend_bothsides_two_kernel(tc, query, cache_words, cache_scales, draft
         picked = sb.tile([P, I], F32, name="picked")
         for h in range(2):
             nc.vector.tensor_copy(picked[:, 256 * h : 256 * (h + 1)], a[:].indirect(l1[:, 16 * h : 16 * (h + 1)]))
-        for h in range(2):
-            nc.scalar.activation(f1[:].indirect(l2[:, 16 * h : 16 * (h + 1)]), picked[:, 256 * h : 256 * (h + 1)], COPY)
-            nc.scalar.activation(f2[:].indirect(l3[:, 16 * h : 16 * (h + 1)]), picked[:, 256 * h : 256 * (h + 1)], COPY)
+        for window, lst, lo, hi in ((f1, l2, 0, 256), (f2, l3, 0, 64), (f1, l2, 256, 512), (f2, l3, 64, 512)):
+            nc.scalar.activation(window[:].indirect(lst[:, lo // 16 : hi // 16]), picked[:, lo:hi], COPY)
 
         minus = sb.tile([P, I], F32, name="minus")
         nc.vector.tensor_copy(minus[:], a[:].indirect(l5[:]))
 
+        diag = sb.tile([P, P], I32, name="diag")
+        nc.gpsimd.iota(diag[:], [[1, P]], base=0, channel_multiplier=-1)
+        ident = sb.tile([P, P], F32, name="ident", tag="d_words", align_bytes=64)
+        nc.vector.tensor_scalar(ident[:], diag[:], 0.0, None, mybir.AluOpType.is_equal)
+        f1_banks = []
+        staged = sb.tile([P, 512], F32, name="staged", tag="bb")
+        for n in range(2):
+            turned = ps.tile([P, 256], F32, name="turned%d" % n, tag="a_bank%d" % n)
+            for j in range(2):
+                nc.tensor.transpose(turned[:, 128 * j : 128 * (j + 1)], f1[:, 256 * n + 128 * j : 256 * n + 128 * (j + 1)], ident[:])
+            nc.vector.tensor_copy(out=staged[:, 256 * n : 256 * (n + 1)], in_=turned[:])
+            back = ps.tile([P, 256], F32, name="back%d" % n, tag="a_bank%d" % (n + 2))
+            for j in range(2):
+                nc.tensor.transpose(back[:, 128 * j : 128 * (j + 1)], staged[:, 256 * n + 128 * j : 256 * n + 128 * (j + 1)], ident[:])
+            f1_banks.append(back)
+
         r = sb.tile([P, U], F32, name="r", tag="a")
         bb = sb.tile([P, U], F32, name="bb")
+        for lo, hi in ((512, 832), (832, 1024)):
+            nc.gpsimd.tensor_tensor(r[:, lo:hi], f1[:, lo:hi], f2[:, lo:hi], SUB)
         for n in range(2):
-            cols = slice(512 * n, 512 * (n + 1))
-            nc.vector.tensor_tensor(r[:, cols], f1[:, cols], f2[:, cols], SUB)
-        for n in range(2):
-            cols = slice(512 * n, 512 * (n + 1))
-            nc.vector.tensor_tensor(bb[:, cols], b_banks[n][:], r[:, cols], MAX)
+            cols = slice(256 * n, 256 * (n + 1))
+            nc.vector.tensor_tensor(r[:, cols], f1_banks[n][:], f2[:, cols], SUB)
+        for lo, hi in ((0, 256), (256, 512), (512, 832), (832, 1024)):
+            nc.vector.tensor_tensor(bb[:, lo:hi], b_banks[lo // 512][:, lo % 512 : lo % 512 + hi - lo], r[:, lo:hi], MAX)
 
         y0 = sb.tile([P, 256], F32, name="y0")
         y1 = sb.tile([P, 256], F32, name="y1")

from contextlib import ExitStack

import concourse.mybir as mybir

F32 = mybir.dt.float32
BF16 = mybir.dt.bfloat16
I32 = mybir.dt.int32
U32 = mybir.dt.uint32
U16 = mybir.dt.uint16
U8 = mybir.dt.uint8
FP8X4 = mybir.dt.float8_e4m3fn_x4
FP4X4 = mybir.dt.float4_e2m1fn_x4
COPY = mybir.ActivationFunctionType.Copy
SUB = mybir.AluOpType.subtract
MAX = mybir.AluOpType.max

P = 128
D, T, U, I, Q = 512, 1024, 1024, 512, 128
FLOPS = 2 * Q * D * (T + U)


def load_scales(nc, queue, plane, scales):
    for quad in range(4):
        queue.dma_start(
            out=plane[32 * quad : 32 * quad + 4, :].bitcast(I32),
            in_=scales[0, 4 * quad : 4 * quad + 4, :].bitcast(I32),
        )


def tile_attend_bothsides_two_kernel(tc, query, cache_words, cache_scales, draft_words, draft_scales, offs, offs2, offs3, offs4, offs5, out):
    nc = tc.nc
    with ExitStack() as ctx:
        sb = ctx.enter_context(tc.tile_pool(name="sb", bufs=1))
        ps = ctx.enter_context(tc.psum_pool(name="ps", bufs=1))

        c_plane = sb.tile([P, T], U8, name="c_plane", align_bytes=64)
        d_plane = sb.tile([P, U], U8, name="d_plane", align_bytes=64)

        q_raw = sb.tile([P, 4, Q], F32, name="q_raw")
        nc.sync.dma_start(out=q_raw[:], in_=query.rearrange("(p j) w -> p j w", j=4))
        c_words = sb.tile([P, 2 * T], U8, name="c_words", align_bytes=64)
        nc.sync.dma_start(out=c_words[:].bitcast(I32), in_=cache_words[0].bitcast(I32))
        load_scales(nc, nc.sync, c_plane, cache_scales)
        lists = []
        for name, src in (("l1", offs), ("l2", offs2), ("l3", offs3), ("l5", offs5)):
            lst = sb.tile([P, I // 16], U16, name=name)
            nc.sync.dma_start(lst[:], src)
            lists.append(lst)
        load_scales(nc, nc.sync, d_plane, draft_scales)
        d_words = sb.tile([P, U], U32, name="d_words", align_bytes=64)
        nc.sync.dma_start(out=d_words[:].bitcast(I32), in_=draft_words[0].rearrange("p n t -> p (n t)").bitcast(I32))
        for name, src in (("l4", offs4),):
            lst = sb.tile([P, I // 16], U16, name=name)
            nc.sync.dma_start(lst[:], src)
            lists.append(lst)
        l1, l2, l3, l5, l4 = lists

        f1 = sb.tile([P, U], F32, name="f1")
        f2 = sb.tile([P, U], F32, name="f2")
        nc.vector.memset(f1[:], 0.0)
        nc.vector.memset(f2[:], 0.0)

        q_bf = sb.tile([P, Q, 4], BF16, name="q_bf", align_bytes=64)
        nc.vector.tensor_copy(out=q_bf[:], in_=q_raw[:].rearrange("p j w -> p w j"))
        q_codes = sb.tile([P, Q], U32, name="q_codes", align_bytes=64)
        q_plane = sb.tile([P, Q], U8, name="q_plane", align_bytes=64)
        nc.vector.quantize_mx(out=q_codes[:].bitcast(FP8X4), scales=q_plane[:], in_=q_bf[:].rearrange("p w j -> p (w j)"))

        a = sb.tile([P, T], F32, name="a")
        start = 0
        for n, width in enumerate((256, 256, 256, 128, 128)):
            bank = ps.tile([P, width], F32, name="a_bank%d" % n)
            nc.tensor.matmul_mx(
                out=bank[:],
                lhsT=q_codes[:].bitcast(FP8X4),
                lhsT_scale=q_plane[:],
                rhs=c_words[:, 2 * start : 2 * (start + width)].bitcast(FP4X4),
                rhs_scale=c_plane[:, start : start + width],
                start=True,
                stop=True,
            )
            if n % 2 == 0:
                nc.scalar.activation(a[:, start : start + width], bank[:], COPY)
            else:
                nc.vector.tensor_copy(out=a[:, start : start + width], in_=bank[:])
            start += width

        b_banks = []
        for n in range(2):
            bank = ps.tile([P, 512], F32, name="b_bank%d" % n)
            nc.tensor.matmul_mx(
                out=bank[:],
                lhsT=q_codes[:].bitcast(FP8X4),
                lhsT_scale=q_plane[:],
                rhs=d_words[:, 512 * n : 512 * (n + 1)].bitcast(FP8X4),
                rhs_scale=d_plane[:, 512 * n : 512 * (n + 1)],
                start=True,
                stop=True,
            )
            b_banks.append(bank)

        picked = sb.tile([P, I], F32, name="picked")
        for h in range(2):
            nc.vector.tensor_copy(picked[:, 256 * h : 256 * (h + 1)], a[:].indirect(l1[:, 16 * h : 16 * (h + 1)]))
        for window, lst, lo, hi in ((f1, l2, 0, 256), (f2, l3, 0, 64), (f1, l2, 256, 512), (f2, l3, 64, 512)):
            nc.scalar.activation(window[:].indirect(lst[:, lo // 16 : hi // 16]), picked[:, lo:hi], COPY)

        minus = sb.tile([P, I], F32, name="minus")
        nc.vector.tensor_copy(minus[:], a[:].indirect(l5[:]))

        diag = sb.tile([P, P], I32, name="diag")
        nc.gpsimd.iota(diag[:], [[1, P]], base=0, channel_multiplier=-1)
        ident = sb.tile([P, P], F32, name="ident", tag="d_words", align_bytes=64)
        nc.vector.tensor_scalar(ident[:], diag[:], 0.0, None, mybir.AluOpType.is_equal)
        f1_banks = []
        staged = sb.tile([P, 512], F32, name="staged", tag="bb")
        for n in range(2):
            turned = ps.tile([P, 256], F32, name="turned%d" % n, tag="a_bank%d" % n)
            for j in range(2):
                nc.tensor.transpose(turned[:, 128 * j : 128 * (j + 1)], f1[:, 256 * n + 128 * j : 256 * n + 128 * (j + 1)], ident[:])
            nc.vector.tensor_copy(out=staged[:, 256 * n : 256 * (n + 1)], in_=turned[:])
            back = ps.tile([P, 256], F32, name="back%d" % n, tag="a_bank%d" % (n + 2))
            for j in range(2):
                nc.tensor.transpose(back[:, 128 * j : 128 * (j + 1)], staged[:, 256 * n + 128 * j : 256 * n + 128 * (j + 1)], ident[:])
            f1_banks.append(back)

        r = sb.tile([P, U], F32, name="r", tag="a")
        bb = sb.tile([P, U], F32, name="bb")
        for lo, hi in ((512, 832), (832, 1024)):
            nc.gpsimd.tensor_tensor(r[:, lo:hi], f1[:, lo:hi], f2[:, lo:hi], SUB)
        for n in range(2):
            cols = slice(256 * n, 256 * (n + 1))
            nc.vector.tensor_tensor(r[:, cols], f1_banks[n][:], f2[:, cols], SUB)
        for lo, hi in ((0, 256), (256, 512), (512, 832), (832, 1024)):
            nc.vector.tensor_tensor(bb[:, lo:hi], b_banks[lo // 512][:, lo % 512 : lo % 512 + hi - lo], r[:, lo:hi], MAX)

        y0 = sb.tile([P, 256], F32, name="y0")
        y1 = sb.tile([P, 256], F32, name="y1")
        g1 = sb.tile([P, 256], F32, name="g1")
        nc.vector.tensor_tensor(y0[:], bb[:].indirect(l4[:, 0:16]), minus[:, 0:256], SUB)
        nc.scalar.activation(g1[:], bb[:].indirect(l4[:, 16:32]), COPY)
        nc.vector.tensor_tensor(y1[:], g1[:], minus[:, 256:512], SUB)
        nc.sync.dma_start(out=out[:, 0:256], in_=y0[:])
        nc.sync.dma_start(out=out[:, 256:512], in_=y1[:])
